import numpy as np
import ml_dtypes


def mxq(x, axis, fmt="e4m3"):
    dtype, down = {"e4m3": (ml_dtypes.float8_e4m3fn, 7), "e5m2": (ml_dtypes.float8_e5m2, 14)}[fmt]
    v = np.moveaxis(np.asarray(x, np.float32).astype(ml_dtypes.bfloat16).astype(np.float64), axis, -1)
    blocks = v.reshape(v.shape[:-1] + (-1, 32))
    amax = np.abs(blocks).max(-1, keepdims=True)
    byte = np.maximum(np.where(amax > 0, np.frexp(amax)[1] - 1 + 127, 0) - down, 1)
    scale = np.exp2(byte - 127.0)
    codes = (blocks / scale).astype(np.float32).astype(dtype).astype(np.float64)
    return np.moveaxis((codes * scale).reshape(v.shape), -1, axis)


WIDE = False


def mx_kscale(k):
    if not WIDE:
        return np.ones(k)
    levels = np.array([10, -10, 5, -5, 0])
    if k % 512:
        return np.exp2(np.random.permutation(np.resize(levels, k // 32))).repeat(32)
    a = np.empty((k // 512, 16))
    for p in range(k // 512):
        a[p, :8] = np.random.permutation(np.resize(levels, 8))
        for g in range(8):
            far = levels[np.abs(levels - a[p, g]) >= 10]
            a[p, g + 8] = far[np.random.randint(len(far))]
    return np.exp2(a.ravel()).repeat(32)


def f64(x):
    return np.asarray(x).astype(np.float64)


def striped(idx):
    return np.tile(idx.reshape(-1, 16).T, (8, 1)).astype(np.uint16)


def unstriped(offs):
    return offs[:16].T.reshape(-1).astype(np.int64)


E2M1 = np.array([0.0, 0.5, 1.0, 1.5, 2.0, 3.0, 4.0, 6.0, -0.0, -0.5, -1.0, -1.5, -2.0, -3.0, -4.0, -6.0])


def pack_weight(w, fmt):
    k, n = w.shape
    w = f64(np.asarray(w, np.float32).astype(ml_dtypes.bfloat16)).reshape(k // 32, 32, n)
    amax = np.abs(w).max(1)
    if fmt == "e4m3":
        byte = np.frexp(amax)[1] - 1 + 127 - 7
    else:
        mant, ex = np.frexp(amax / 6.0)
        byte = np.where(mant > 0.5, ex, ex - 1) + 127
    byte = np.clip(np.where(amax > 0, byte, 1), 1, 254)
    scaled = (w * np.exp2(127.0 - byte)[:, None, :]).reshape(k, n).astype(np.float32)
    by_word = np.ascontiguousarray(scaled.reshape(k // 512, 128, 4, n).transpose(0, 1, 3, 2))
    if fmt == "e4m3":
        words = by_word.astype(ml_dtypes.float8_e4m3fn).view(np.uint8)
    else:
        c = by_word.astype(ml_dtypes.float4_e2m1fn).view(np.uint8) & 0xF
        words = (c[..., 0::2] | (c[..., 1::2] << 4)).reshape(k // 512, 128, 2 * n)
    return np.ascontiguousarray(words), np.ascontiguousarray(byte.astype(np.uint8).reshape(k // 512, 16, n))


def unpack_weight(words, scales, fmt):
    g, _, n = scales.shape
    words = np.ascontiguousarray(words).reshape(g, 128, n, -1)
    if fmt == "e4m3":
        vals = words.view(ml_dtypes.float8_e4m3fn).astype(np.float64)
    else:
        nib = np.empty((g, 128, n, 4), np.uint8)
        nib[..., 0::2] = words & 0xF
        nib[..., 1::2] = words >> 4
        vals = E2M1[nib]
    vals = vals * np.repeat(np.exp2(scales.astype(np.float64) - 127.0), 8, axis=1)[..., None]
    return vals.transpose(0, 1, 3, 2).reshape(g * 512, n)


def gelu(v):
    return 0.5 * v * (1.0 + np.tanh(np.sqrt(2.0 / np.pi) * (v + 0.044715 * v**3)))


K, T, S, H, T2, P = 1024, 2048, 512, 1024, 1024, 512

def setup_inputs():
    n = np.random.standard_normal
    s = mx_kscale(K)[:, None]
    u = mx_kscale(H)[:, None]
    d = {}
    d["tab_words"], d["tab_scales"] = pack_weight(n((K, T)) * s, "e4m3")
    d["offs"] = striped(np.random.permutation(T)[:S])
    d["offs2"] = striped(np.random.permutation(T2)[:S])
    d["offs3"] = striped(np.random.permutation(T2)[:P])
    d["w1"] = (0.7 * n((K, H)) / K ** 0.5 / s * np.sqrt(u).T).astype(np.float32)
    d["clutter"] = (0.5 * n((H, S)) * np.sqrt(u)).astype(np.float32)
    d["w4_words"], d["w4_scales"] = pack_weight(0.8 * n((K, H)) / K ** 0.5 / s * u.T, "e2m1")
    d["wgs"] = np.exp(0.3 * n((128, S))).astype(np.float32)
    d["page0"] = (1.2 * n((H, T2)) * u).astype(np.float32)
    d["hazard"] = (n(H) / (u[:, 0] ** 2 * H ** 0.5)).astype(np.float32)
    d["slot"] = (0.6 * np.exp(0.3 * n(T2))).astype(np.float32)
    d["floors"] = n((T2, P)).astype(np.float32)
    return d

def reference(tab_words, tab_scales, offs, offs2, offs3, w1, clutter, w4_words, w4_scales, wgs, page0, hazard, slot, floors):
    v = unpack_weight(tab_words, tab_scales, "e4m3")[:, unstriped(offs)]
    w4 = unpack_weight(w4_words, w4_scales, "e2m1")
    a = mxq(f64(w1), 0, "e4m3").T @ v
    b = w4.T @ v
    h = np.square(a - f64(clutter)) + b
    page = f64(page0).copy()
    page[:, unstriped(offs2)] = np.tile(f64(wgs), (H // 128, 1)) * h
    x = np.abs(page[:, unstriped(offs3)]) * f64(hazard)[:, None]
    e = mxq(page, 0, "e4m3").T @ mxq(x, 0, "e4m3")
    return np.maximum(e * f64(slot)[:, None], f64(floors))

@@ -1,0 +1,328 @@
+from contextlib import ExitStack
+
+import concourse.mybir as mybir
+from concourse.masks import make_identity
+
+K, T, S, H, T2, NX = 1024, 2048, 512, 1024, 1024, 512
+FLOPS = 2 * (2 * K * H * S + H * T2 * NX)
+
+F32 = mybir.dt.float32
+BF16 = mybir.dt.bfloat16
+I32 = mybir.dt.int32
+U32 = mybir.dt.uint32
+U16 = mybir.dt.uint16
+U8 = mybir.dt.uint8
+FP8X4 = mybir.dt.float8_e4m3fn_x4
+FP4X4 = mybir.dt.float4_e2m1fn_x4
+ALU = mybir.AluOpType
+ACT = mybir.ActivationFunctionType
+
+P = 128
+PASSES = 2
+SLICES = H // P
+W4_CHUNKS = ((0, 2), (2, 8))
+W1_CHUNKS = ((0, 1), (1, 3), (3, 5), (5, 8))
+
+
+def tile_list_flock_page_alerts_kernel(
+    tc, tab_words, tab_scales, offs, offs2, offs3, w1, clutter, w4_words, w4_scales, wgs, page0, hazard, slot, floors, out
+):
+    nc = tc.nc
+    with ExitStack() as ctx:
+        keep = ctx.enter_context(tc.tile_pool(name="keep", bufs=1))
+        ring = ctx.enter_context(tc.tile_pool(name="ring", bufs=2))
+        banks = ctx.enter_context(tc.psum_pool(name="banks", bufs=1))
+
+        list1 = keep.tile([P, S // 16], U16, name="list1")
+        list2 = keep.tile([P, S // 16], U16, name="list2")
+        list3 = keep.tile([P, NX // 16], U16, name="list3")
+        tab_w = [keep.tile([P, T], I32, name="tab_w%d" % a, tag="big%d" % a) for a in range(PASSES)]
+        tab_s = keep.tile([P, T], U8, name="tab_s")
+        v_w = [keep.tile([P, S], U32, name="v_w%d" % a, align_bytes=64) for a in range(PASSES)]
+        v_s = keep.tile([P, S], U8, name="v_s", align_bytes=64)
+        v_s1 = keep.tile([P, S], U8, name="v_s1", align_bytes=64)
+        w4_w = [keep.tile([P, PASSES, 2 * P * (hi - lo)], U8, name="w4_w%d" % lo, align_bytes=64) for lo, hi in W4_CHUNKS]
+        w4_s = keep.tile([P, PASSES, H], U8, name="w4_s", align_bytes=64)
+        w1_raw = [
+            [keep.tile([P, 4, P * (hi - lo)], F32, name="w1_raw%d_%d" % (lo, a)) for a in range(PASSES)]
+            for lo, hi in W1_CHUNKS
+        ]
+        w1_s = [keep.tile([P, PASSES * P], U8, name="w1_s%d" % s, align_bytes=64) for s in range(SLICES)]
+        clut = [keep.tile([P, S], F32, name="clut%d" % s, tag="row%d" % s, align_bytes=64) for s in range(SLICES)]
+        gain = keep.tile([P, S], F32, name="gain")
+        page = [keep.tile([P, T2], F32, name="page%d" % s) for s in range(SLICES)]
+        vec_rows = keep.tile([P, P], F32, name="vec_rows")
+        vec_cols = keep.tile([P, 16], F32, name="vec_cols")
+        ident32 = keep.tile([P, P], F32, name="ident32")
+        ident16 = keep.tile([P, P], BF16, name="ident16")
+        page_s = [[keep.tile([P, 512], U8, name="page_s%d_%d" % (b, hf), align_bytes=64) for hf in range(2)] for b in range(PASSES)]
+        x_s = [keep.tile([P, NX], U8, name="x_s%d" % b, align_bytes=64) for b in range(PASSES)]
+
+        nc.gpsimd.memset(tab_s[:].bitcast(I32), 0)
+        nc.vector.memset(w4_s[:].rearrange("p a t -> p (a t)").bitcast(I32), 0)
+        nc.vector.memset(v_s1[:].bitcast(I32), 0)
+
+        def load_w1(c, *passes):
+            for a in passes or range(PASSES):
+                nc.sync.dma_start(
+                    out=w1_raw[c][a][:],
+                    in_=w1[512 * a : 512 * (a + 1), P * W1_CHUNKS[c][0] : P * W1_CHUNKS[c][1]].rearrange("(p j) c -> p j c", j=4),
+                )
+
+        def load_clutter(s):
+            nc.sync.dma_start(out=clut[s][:], in_=clutter[P * s : P * (s + 1), :])
+
+        def load_page(s):
+            nc.sync.dma_start(out=page[s][:], in_=page0[P * s : P * (s + 1), :])
+
+        def load_w4(c):
+            lo, hi = W4_CHUNKS[c]
+            nc.sync.dma_start(
+                out=w4_w[c][:].bitcast(I32),
+                in_=w4_words.rearrange("a p n -> p a n")[:, :, 2 * P * lo : 2 * P * hi].bitcast(I32),
+            )
+
+        nc.gpsimd.memset(vec_rows[:], 0.0)
+        make_identity(nc, ident32[:])
+        make_identity(nc, ident16[:])
+        nc.gpsimd.dma_start(out=vec_rows[0:8, :], in_=hazard.rearrange("(s p) -> s p", p=P))
+        nc.gpsimd.dma_start(out=vec_rows[8:16, :], in_=slot.rearrange("(s p) -> s p", p=P))
+        nc.sync.dma_start(list1[:], offs)
+        load_w1(0, 0)
+        for q in range(4):
+            nc.sync.dma_start(
+                out=tab_s[32 * q : 32 * q + 8, :].bitcast(I32), in_=tab_scales[:, 4 * q : 4 * q + 4, :].bitcast(I32)
+            )
+        load_w1(0, 1)
+        for a in range(PASSES):
+            nc.sync.dma_start(out=tab_w[a][:], in_=tab_words[a].rearrange("p t i -> p (t i)").bitcast(I32))
+        for q in range(4):
+            nc.sync.dma_start(
+                out=w4_s[32 * q : 32 * q + 4, :, :].bitcast(I32),
+                in_=w4_scales[:, 4 * q : 4 * q + 4, :].rearrange("a q t -> q a t").bitcast(I32),
+            )
+        load_w4(0)
+        load_clutter(0)
+        nc.sync.dma_start(out=gain[:], in_=wgs)
+        load_page(0)
+        nc.sync.dma_start(list2[:], offs2)
+        nc.sync.dma_start(list3[:], offs3)
+        load_w1(1)
+        load_w4(1)
+        load_clutter(1)
+        load_clutter(2)
+        load_w1(2)
+        load_page(1)
+        load_clutter(3)
+        load_page(2)
+        load_w1(3)
+        for s in range(3, SLICES):
+            if s + 1 < SLICES:
+                load_clutter(s + 1)
+            load_page(s)
+
+        nc.vector.tensor_copy(v_s[:], tab_s[:].indirect(list1[:]))
+
+        w1_woven = {}
+
+        def diff_tag(s):
+            return "row%d" % (s - 1 if s >= 2 else SLICES + 1 + s)
+
+        def weave_tag(s):
+            return diff_tag(s - 2) if s >= 2 else ("weave0", "row0")[s]
+
+        def weave_w1(s):
+            c = [lo <= s < hi for lo, hi in W1_CHUNKS].index(True)
+            c0 = P * (s - W1_CHUNKS[c][0])
+            woven = keep.tile([P, PASSES, P * 4], BF16, name="w1_woven", tag=weave_tag(s), align_bytes=64)
+            for a in range(PASSES):
+                dst = woven[:, a, :].rearrange("p (c i j) -> p c j i", i=4, j=4)
+                src = w1_raw[c][a][:, :, c0 : c0 + P].rearrange("p j (c i) -> p c j i", i=4)
+                nc.scalar.copy(dst, src)
+            w1_woven[s] = woven
+
+        w1_w = {}
+
+        def quantise_w1(s):
+            w1_w[s] = keep.tile([P, PASSES * P], U32, name="w1_w", tag="size%d" % (s - 3), align_bytes=64)
+            nc.vector.quantize_mx(out=w1_w[s][:].bitcast(FP8X4), scales=w1_s[s][:], in_=w1_woven[s][:].rearrange("p a n -> p (a n)"))
+
+        weave_w1(0)
+        for q in range(4):
+            nc.scalar.dma_start(out=v_s1[32 * q : 32 * q + 4, :].bitcast(I32), in_=v_s[32 * q + 4 : 32 * q + 8, :].bitcast(I32))
+        quantise_w1(0)
+        for a in range(PASSES):
+            nc.vector.tensor_copy(v_w[a][:], tab_w[a][:].bitcast(U32).indirect(list1[:]))
+
+        vec_bank = banks.tile([P, P], F32, name="vec_bank", tag="x")
+        nc.tensor.transpose(vec_bank[:], vec_rows[:], ident32[:])
+        nc.scalar.copy(vec_cols[:], vec_bank[:, 0:16])
+
+        diffs = {}
+        squares = {}
+        feats = {}
+        sizes = {}
+        xs = {}
+        page_t = {}
+        x_t = {}
+
+        def departure(s):
+            a_bank = banks.tile([P, S], F32, name="a_bank", tag="c" if s == 1 else "a")
+            for a in range(PASSES):
+                nc.tensor.matmul_mx(
+                    out=a_bank[:],
+                    lhsT=w1_w[s][:, P * a : P * (a + 1)].bitcast(FP8X4),
+                    lhsT_scale=w1_s[s][:, P * a : P * (a + 1)],
+                    rhs=v_w[a][:].bitcast(FP8X4),
+                    rhs_scale=v_s[4 * a :, :],
+                    start=(a == 0),
+                    stop=(a == PASSES - 1),
+                )
+            diffs[s] = keep.tile([P, S], F32, name="diff", tag=diff_tag(s), align_bytes=64)
+            nc.vector.tensor_tensor(diffs[s][:], a_bank[:], clut[s][:], ALU.subtract)
+
+        def square(s):
+            squares[s] = ring.tile([P, S], F32, name="squared")
+            nc.scalar.activation(squares[s][:], diffs[s][:], ACT.Square)
+
+        def feature(s):
+            c = [lo <= s < hi for lo, hi in W4_CHUNKS].index(True)
+            at = s - W4_CHUNKS[c][0]
+            b_bank = banks.tile([P, S], F32, name="b_bank", tag="b")
+            for a in range(PASSES):
+                nc.tensor.matmul_mx(
+                    out=b_bank[:],
+                    lhsT=w4_w[c][:, a, 2 * P * at : 2 * P * (at + 1)].bitcast(FP4X4),
+                    lhsT_scale=w4_s[:, a, P * s : P * (s + 1)],
+                    rhs=v_w[a][:].bitcast(FP8X4),
+                    rhs_scale=(v_s, v_s1)[a][:],
+                    start=(a == 0),
+                    stop=(a == PASSES - 1),
+                )
+            feats[s] = keep.tile([P, S], F32, name="feat", tag="row%d" % (s + 1 if s >= 1 else SLICES + 3), align_bytes=64)
+            nc.vector.tensor_tensor(feats[s][:], b_bank[:], squares[s][:], ALU.add)
+
+        def put(s):
+            nc.vector.tensor_tensor(page[s][:].indirect(list2[:]), feats[s][:], gain[:], ALU.mult)
+
+        def turn_page(s, tags, copy):
+            sl = s % 4
+            for hf in range(2):
+                if sl == 0:
+                    page_t[s // 4, hf] = ring.tile([P, 2048], BF16, name="page_t", tag="page_t%d" % hf)
+                bank = banks.tile([P, 4, P], F32, name="page_bank", tag=tags[hf])
+                for mt in range(4):
+                    c0 = P * (4 * hf + mt)
+                    nc.tensor.transpose(bank[:, mt, :], page[s][:, c0 : c0 + P], ident32[:])
+                copy(
+                    page_t[s // 4, hf][:].rearrange("m (c u p e) -> m c u p e", c=4, u=2, e=2)[:, :, :, 32 * sl : 32 * sl + 32, :],
+                    bank[:].rearrange("m c (p u e) -> m c u p e", u=2, e=2),
+                )
+
+        def fetch(s):
+            picked = keep.tile([P, NX], F32, name="picked", tag=weave_tag((s + 2) % SLICES), align_bytes=64)
+            nc.vector.tensor_copy(picked[:], page[s][:].indirect(list3[:]))
+            sizes[s] = keep.tile([P, NX], F32, name="size", tag="size%d" % s, align_bytes=64)
+            nc.scalar.activation(sizes[s][:], picked[:], ACT.Abs)
+
+        def weigh(s):
+            xs[s] = ring.tile([P, NX], BF16, name="x")
+            nc.scalar.activation(xs[s][:], sizes[s][:], ACT.Copy, scale=vec_cols[:, s : s + 1])
+
+        def turn_x(s):
+            sl = s % 4
+            if sl == 0:
+                x_t[s // 4] = ring.tile([P, 2048], BF16, name="x_t", tag="x_t")
+            bank = banks.tile([P, 4, P], BF16, name="x_bank", tag="x")
+            for nt in range(4):
+                nc.tensor.transpose(bank[:, nt, :], xs[s][:, P * nt : P * (nt + 1)], ident16[:])
+            nc.scalar.copy(
+                x_t[s // 4][:].bitcast(F32).rearrange("n (c u p) -> n c u p", c=4, u=2)[:, :, :, 32 * sl : 32 * sl + 32],
+                bank[:].bitcast(F32).rearrange("n c (p u) -> n c u p", u=2),
+            )
+
+        def turn_back(turned, name, copies):
+            words = turned[:].bitcast(F32).rearrange("m (c u p) -> m c u p", c=4, u=2)
+            woven = keep.tile([P, 2048], BF16, name=name, align_bytes=64)
+            woven_words = woven[:].bitcast(F32).rearrange("p (c m u) -> p c m u", c=4, u=2)
+            for pair in range(2):
+                bank = banks.tile([P, 2, 2, P], F32, name="back_bank", tag="back", bufs=3)
+                for c in range(2):
+                    for u in range(2):
+                        nc.tensor.transpose(bank[:, c, u, :], words[:, 2 * pair + c, u, :], ident32[:])
+                copies[pair](woven_words[:, 2 * pair : 2 * pair + 2, :, :], bank[:].rearrange("p c u m -> p c m u"))
+            return woven
+
+        def quantise(codes, scales, woven):
+            nc.vector.quantize_mx(out=codes.bitcast(FP8X4), scales=scales[:], in_=woven[:])
+
+        on_scalar = nc.scalar.copy
+        on_vector = nc.vector.tensor_copy
+        both_on_scalar = (on_scalar, on_scalar)
+        departure(0)
+        square(0)
+        weave_w1(1)
+        weave_w1(2)
+        feature(0)
+        woven0 = []
+        for s in range(SLICES):
+            put(s)
+            if s == 0:
+                quantise_w1(1)
+            if s + 2 < SLICES:
+                quantise_w1(s + 2)
+            fetch(s)
+            if s == 0:
+                departure(1)
+                square(1)
+                weave_w1(3)
+            if s + 2 < SLICES:
+                departure(s + 2)
+                square(s + 2)
+            weigh(s)
+            if s + 1 < SLICES:
+                feature(s + 1)
+                turn_page(s, "ax", on_scalar)
+            if s + 4 < SLICES:
+                weave_w1(s + 4)
+            turn_x(s)
+            if 4 <= s < 7:
+                woven0.append(turn_back((page_t[0, 0], page_t[0, 1], x_t[0])[s - 4], "woven0%d" % (s - 4), both_on_scalar))
+
+        turn_page(SLICES - 1, "cd", on_vector)
+        codes = [
+            keep.tile([P, 3, 512], U32, name="codes0", tag="row8", align_bytes=64),
+            keep.tile([P, 3, 512], U32, name="codes1", align_bytes=64),
+        ]
+        for hf in range(2):
+            quantise(codes[0][:, hf, :], page_s[0][hf], woven0[hf])
+        quantise(codes[0][:, 2, :], x_s[0], woven0[2])
+        page_woven = turn_back(page_t[1, 0], "page_woven10", both_on_scalar)
+        x_woven = turn_back(x_t[1], "x_woven1", (on_scalar, on_vector))
+        quantise(codes[1][:, 0, :], page_s[1][0], page_woven)
+        quantise(codes[1][:, 2, :], x_s[1], x_woven)
+        page_woven = turn_back(page_t[1, 1], "page_woven11", both_on_scalar)
+        quantise(codes[1][:, 1, :], page_s[1][1], page_woven)
+
+        floor = [keep.tile([P, 4, NX], F32, name="floor%d" % hf, tag="big%d" % hf) for hf in range(2)]
+        for hf in range(2):
+            nc.sync.dma_start(
+                out=floor[hf][:], in_=floors[512 * hf : 512 * (hf + 1), :].rearrange("(s p) n -> p s n", p=P)
+            )
+
+        for mt in range(T2 // P):
+            hf, c = divmod(mt, 4)
+            e_bank = banks.tile([P, NX], F32, name="e_bank", tag="abcd"[mt % 4])
+            for b in reversed(range(PASSES)):
+                nc.tensor.matmul_mx(
+                    out=e_bank[:],
+                    lhsT=codes[b][:, hf, P * c : P * (c + 1)].bitcast(FP8X4),
+                    lhsT_scale=page_s[b][hf][:, P * c : P * (c + 1)],
+                    rhs=codes[b][:, 2, :].bitcast(FP8X4),
+                    rhs_scale=x_s[b][:],
+                    start=(b == PASSES - 1),
+                    stop=(b == 0),
+                )
+            alert = keep.tile([P, NX], F32, name="alert", tag="alert", bufs=4)
+            nc.vector.scalar_tensor_tensor(alert[:], e_bank[:], vec_cols[:, 8 + mt : 9 + mt], floor[hf][:, c, :], ALU.mult, ALU.max)
+            nc.sync.dma_start(out=out[P * mt : P * (mt + 1), :], in_=alert[:])

@@ -21,7 +21,7 @@ P = 128
 PASSES = 2
 SLICES = H // P
 W4_CHUNKS = ((0, 2), (2, 8))
-W1_CHUNKS = ((0, 1), (1, 3), (3, 5), (5, 8))
+W1_CHUNKS = ((0, 2), (2, 4), (4, 6), (6, 8))
 
 
 def tile_list_flock_page_alerts_kernel(
@@ -37,14 +37,13 @@ def tile_list_flock_page_alerts_kernel(
         list2 = keep.tile([P, S // 16], U16, name="list2")
         list3 = keep.tile([P, NX // 16], U16, name="list3")
         tab_w = [keep.tile([P, T], I32, name="tab_w%d" % a, tag="big%d" % a) for a in range(PASSES)]
-        tab_s = keep.tile([P, T], U8, name="tab_s")
+        tab_s = keep.tile([P, PASSES, T], U8, name="tab_s")
         v_w = [keep.tile([P, S], U32, name="v_w%d" % a, align_bytes=64) for a in range(PASSES)]
-        v_s = keep.tile([P, S], U8, name="v_s", align_bytes=64)
-        v_s1 = keep.tile([P, S], U8, name="v_s1", align_bytes=64)
+        v_s = [keep.tile([P, S], U8, name="v_s%d" % a, align_bytes=64) for a in range(PASSES)]
         w4_w = [keep.tile([P, PASSES, 2 * P * (hi - lo)], U8, name="w4_w%d" % lo, align_bytes=64) for lo, hi in W4_CHUNKS]
         w4_s = keep.tile([P, PASSES, H], U8, name="w4_s", align_bytes=64)
         w1_raw = [
-            [keep.tile([P, 4, P * (hi - lo)], F32, name="w1_raw%d_%d" % (lo, a)) for a in range(PASSES)]
+            [keep.tile([P, 4, P * (hi - lo)], F32, name="w1_raw", tag="raw%d" % (lo + a), align_bytes=64) for a in range(PASSES)]
             for lo, hi in W1_CHUNKS
         ]
         w1_s = [keep.tile([P, PASSES * P], U8, name="w1_s%d" % s, align_bytes=64) for s in range(SLICES)]
@@ -58,9 +57,15 @@ def tile_list_flock_page_alerts_kernel(
         page_s = [[keep.tile([P, 512], U8, name="page_s%d_%d" % (b, hf), align_bytes=64) for hf in range(2)] for b in range(PASSES)]
         x_s = [keep.tile([P, NX], U8, name="x_s%d" % b, align_bytes=64) for b in range(PASSES)]
 
-        nc.gpsimd.memset(tab_s[:].bitcast(I32), 0)
+        nc.gpsimd.memset(tab_s[:].rearrange("p a t -> p (a t)").bitcast(I32), 0)
         nc.vector.memset(w4_s[:].rearrange("p a t -> p (a t)").bitcast(I32), 0)
-        nc.vector.memset(v_s1[:].bitcast(I32), 0)
+
+        def load_scales(queue, tile, src):
+            for q in range(4):
+                queue.dma_start(
+                    out=tile[32 * q : 32 * q + 4, :, :].bitcast(I32),
+                    in_=src[:, 4 * q : 4 * q + 4, :].rearrange("a q t -> q a t").bitcast(I32),
+                )
 
         def load_w1(c, *passes):
             for a in passes or range(PASSES):
@@ -89,39 +94,35 @@ def tile_list_flock_page_alerts_kernel(
         nc.gpsimd.dma_start(out=vec_rows[8:16, :], in_=slot.rearrange("(s p) -> s p", p=P))
         nc.sync.dma_start(list1[:], offs)
         load_w1(0, 0)
-        for q in range(4):
-            nc.sync.dma_start(
-                out=tab_s[32 * q : 32 * q + 8, :].bitcast(I32), in_=tab_scales[:, 4 * q : 4 * q + 4, :].bitcast(I32)
-            )
+        load_scales(nc.sync, tab_s, tab_scales)
         load_w1(0, 1)
         for a in range(PASSES):
             nc.sync.dma_start(out=tab_w[a][:], in_=tab_words[a].rearrange("p t i -> p (t i)").bitcast(I32))
-        for q in range(4):
-            nc.sync.dma_start(
-                out=w4_s[32 * q : 32 * q + 4, :, :].bitcast(I32),
-                in_=w4_scales[:, 4 * q : 4 * q + 4, :].rearrange("a q t -> q a t").bitcast(I32),
-            )
+        load_scales(nc.sync, w4_s, w4_scales)
         load_w4(0)
         load_clutter(0)
+        load_clutter(1)
         nc.sync.dma_start(out=gain[:], in_=wgs)
         load_page(0)
         nc.sync.dma_start(list2[:], offs2)
         nc.sync.dma_start(list3[:], offs3)
         load_w1(1)
-        load_w4(1)
-        load_clutter(1)
         load_clutter(2)
-        load_w1(2)
         load_page(1)
+        load_w4(1)
         load_clutter(3)
+        load_w1(2)
         load_page(2)
+        load_clutter(4)
+        load_page(3)
         load_w1(3)
-        for s in range(3, SLICES):
+        for s in range(4, SLICES):
             if s + 1 < SLICES:
                 load_clutter(s + 1)
             load_page(s)
 
-        nc.vector.tensor_copy(v_s[:], tab_s[:].indirect(list1[:]))
+        for a in range(PASSES):
+            nc.vector.tensor_copy(v_s[a][:], tab_s[:, a, :].indirect(list1[:]))
 
         w1_woven = {}
 
@@ -129,7 +130,7 @@ def tile_list_flock_page_alerts_kernel(
             return "row%d" % (s - 1 if s >= 2 else SLICES + 1 + s)
 
         def weave_tag(s):
-            return diff_tag(s - 2) if s >= 2 else ("weave0", "row0")[s]
+            return diff_tag(s - 2) if s >= 2 else "weave%d" % s
 
         def weave_w1(s):
             c = [lo <= s < hi for lo, hi in W1_CHUNKS].index(True)
@@ -147,10 +148,9 @@ def tile_list_flock_page_alerts_kernel(
             w1_w[s] = keep.tile([P, PASSES * P], U32, name="w1_w", tag="size%d" % (s - 3), align_bytes=64)
             nc.vector.quantize_mx(out=w1_w[s][:].bitcast(FP8X4), scales=w1_s[s][:], in_=w1_woven[s][:].rearrange("p a n -> p (a n)"))
 
-        weave_w1(0)
-        for q in range(4):
-            nc.scalar.dma_start(out=v_s1[32 * q : 32 * q + 4, :].bitcast(I32), in_=v_s[32 * q + 4 : 32 * q + 8, :].bitcast(I32))
-        quantise_w1(0)
+        for s in range(2):
+            weave_w1(s)
+            quantise_w1(s)
         for a in range(PASSES):
             nc.vector.tensor_copy(v_w[a][:], tab_w[a][:].bitcast(U32).indirect(list1[:]))
 
@@ -174,7 +174,7 @@ def tile_list_flock_page_alerts_kernel(
                     lhsT=w1_w[s][:, P * a : P * (a + 1)].bitcast(FP8X4),
                     lhsT_scale=w1_s[s][:, P * a : P * (a + 1)],
                     rhs=v_w[a][:].bitcast(FP8X4),
-                    rhs_scale=v_s[4 * a :, :],
+                    rhs_scale=v_s[a][:],
                     start=(a == 0),
                     stop=(a == PASSES - 1),
                 )
@@ -188,18 +188,18 @@ def tile_list_flock_page_alerts_kernel(
         def feature(s):
             c = [lo <= s < hi for lo, hi in W4_CHUNKS].index(True)
             at = s - W4_CHUNKS[c][0]
-            b_bank = banks.tile([P, S], F32, name="b_bank", tag="b")
+            b_bank = banks.tile([P, S], F32, name="b_bank", tag="b%d" % (s % 2))
             for a in range(PASSES):
                 nc.tensor.matmul_mx(
                     out=b_bank[:],
                     lhsT=w4_w[c][:, a, 2 * P * at : 2 * P * (at + 1)].bitcast(FP4X4),
                     lhsT_scale=w4_s[:, a, P * s : P * (s + 1)],
                     rhs=v_w[a][:].bitcast(FP8X4),
-                    rhs_scale=(v_s, v_s1)[a][:],
+                    rhs_scale=v_s[a][:],
                     start=(a == 0),
                     stop=(a == PASSES - 1),
                 )
-            feats[s] = keep.tile([P, S], F32, name="feat", tag="row%d" % (s + 1 if s >= 1 else SLICES + 3), align_bytes=64)
+            feats[s] = keep.tile([P, S], F32, name="feat", tag="row%d" % (s + 1), align_bytes=64)
             nc.vector.tensor_tensor(feats[s][:], b_bank[:], squares[s][:], ALU.add)
 
         def put(s):
@@ -220,7 +220,7 @@ def tile_list_flock_page_alerts_kernel(
                 )
 
         def fetch(s):
-            picked = keep.tile([P, NX], F32, name="picked", tag=weave_tag((s + 2) % SLICES), align_bytes=64)
+            picked = keep.tile([P, NX], F32, name="picked", tag=weave_tag(s + 2) if s + 2 < SLICES else "size%d" % (s - 1), align_bytes=64)
             nc.vector.tensor_copy(picked[:], page[s][:].indirect(list3[:]))
             sizes[s] = keep.tile([P, NX], F32, name="size", tag="size%d" % s, align_bytes=64)
             nc.scalar.activation(sizes[s][:], picked[:], ACT.Abs)
@@ -233,7 +233,7 @@ def tile_list_flock_page_alerts_kernel(
             sl = s % 4
             if sl == 0:
                 x_t[s // 4] = ring.tile([P, 2048], BF16, name="x_t", tag="x_t")
-            bank = banks.tile([P, 4, P], BF16, name="x_bank", tag="x")
+            bank = banks.tile([P, 4, P], BF16, name="x_bank", tag="x" if s + 1 < SLICES else "c")
             for nt in range(4):
                 nc.tensor.transpose(bank[:, nt, :], xs[s][:, P * nt : P * (nt + 1)], ident16[:])
             nc.scalar.copy(
@@ -243,7 +243,7 @@ def tile_list_flock_page_alerts_kernel(
 
         def turn_back(turned, name, copies):
             words = turned[:].bitcast(F32).rearrange("m (c u p) -> m c u p", c=4, u=2)
-            woven = keep.tile([P, 2048], BF16, name=name, align_bytes=64)
+            woven = keep.tile([P, 2048], BF16, name="woven", tag=name, align_bytes=64)
             woven_words = woven[:].bitcast(F32).rearrange("p (c m u) -> p c m u", c=4, u=2)
             for pair in range(2):
                 bank = banks.tile([P, 2, 2, P], F32, name="back_bank", tag="back", bufs=3)
@@ -259,37 +259,32 @@ def tile_list_flock_page_alerts_kernel(
         on_scalar = nc.scalar.copy
         on_vector = nc.vector.tensor_copy
         both_on_scalar = (on_scalar, on_scalar)
-        departure(0)
-        square(0)
-        weave_w1(1)
-        weave_w1(2)
+        for s in range(2):
+            departure(s)
+            square(s)
         feature(0)
+        weave_w1(2)
+        weave_w1(3)
         woven0 = []
         for s in range(SLICES):
             put(s)
-            if s == 0:
-                quantise_w1(1)
             if s + 2 < SLICES:
                 quantise_w1(s + 2)
             fetch(s)
-            if s == 0:
-                departure(1)
-                square(1)
-                weave_w1(3)
             if s + 2 < SLICES:
                 departure(s + 2)
                 square(s + 2)
             weigh(s)
             if s + 1 < SLICES:
                 feature(s + 1)
-                turn_page(s, "ax", on_scalar)
+                turn_page(s, ("a" if s + 2 < SLICES else "x", "b%d" % ((s + 1) % 2)), on_scalar)
             if s + 4 < SLICES:
                 weave_w1(s + 4)
             turn_x(s)
             if 4 <= s < 7:
-                woven0.append(turn_back((page_t[0, 0], page_t[0, 1], x_t[0])[s - 4], "woven0%d" % (s - 4), both_on_scalar))
+                woven0.append(turn_back((page_t[0, 0], page_t[0, 1], x_t[0])[s - 4], "raw%d" % (s - 4), both_on_scalar))
 
-        turn_page(SLICES - 1, "cd", on_vector)
+        turn_page(SLICES - 1, ("x", "b1"), on_vector)
         codes = [
             keep.tile([P, 3, 512], U32, name="codes0", tag="row8", align_bytes=64),
             keep.tile([P, 3, 512], U32, name="codes1", align_bytes=64),
@@ -297,11 +292,11 @@ def tile_list_flock_page_alerts_kernel(
         for hf in range(2):
             quantise(codes[0][:, hf, :], page_s[0][hf], woven0[hf])
         quantise(codes[0][:, 2, :], x_s[0], woven0[2])
-        page_woven = turn_back(page_t[1, 0], "page_woven10", both_on_scalar)
-        x_woven = turn_back(x_t[1], "x_woven1", (on_scalar, on_vector))
+        page_woven = turn_back(page_t[1, 0], "raw3", both_on_scalar)
+        x_woven = turn_back(x_t[1], "raw4", (on_scalar, on_vector))
         quantise(codes[1][:, 0, :], page_s[1][0], page_woven)
         quantise(codes[1][:, 2, :], x_s[1], x_woven)
-        page_woven = turn_back(page_t[1, 1], "page_woven11", both_on_scalar)
+        page_woven = turn_back(page_t[1, 1], "raw5", both_on_scalar)
         quantise(codes[1][:, 1, :], page_s[1][1], page_woven)
 
         floor = [keep.tile([P, 4, NX], F32, name="floor%d" % hf, tag="big%d" % hf) for hf in range(2)]
@@ -312,7 +307,7 @@ def tile_list_flock_page_alerts_kernel(
 
         for mt in range(T2 // P):
             hf, c = divmod(mt, 4)
-            e_bank = banks.tile([P, NX], F32, name="e_bank", tag="abcd"[mt % 4])
+            e_bank = banks.tile([P, NX], F32, name="e_bank", tag=("a", "b0", "x", "b1")[mt % 4])
             for b in reversed(range(PASSES)):
                 nc.tensor.matmul_mx(
                     out=e_bank[:],
@@ -323,6 +318,6 @@ def tile_list_flock_page_alerts_kernel(
                     start=(b == PASSES - 1),
                     stop=(b == 0),
                 )
-            alert = keep.tile([P, NX], F32, name="alert", tag="alert", bufs=4)
+            alert = keep.tile([P, NX], F32, name="alert%d" % mt)
             nc.vector.scalar_tensor_tensor(alert[:], e_bank[:], vec_cols[:, 8 + mt : 9 + mt], floor[hf][:, c, :], ALU.mult, ALU.max)
             nc.sync.dma_start(out=out[P * mt : P * (mt + 1), :], in_=alert[:])

@@ -145,7 +145,7 @@ def tile_list_flock_page_alerts_kernel(
         w1_w = {}
 
         def quantise_w1(s):
-            w1_w[s] = keep.tile([P, PASSES * P], U32, name="w1_w", tag="size%d" % (s - 3), align_bytes=64)
+            w1_w[s] = keep.tile([P, PASSES * P], U32, name="w1_w", tag="size-1" if s == 3 else "w1_w%d" % s, align_bytes=64)
             nc.vector.quantize_mx(out=w1_w[s][:].bitcast(FP8X4), scales=w1_s[s][:], in_=w1_woven[s][:].rearrange("p a n -> p (a n)"))
 
         for s in range(2):
@@ -220,7 +220,7 @@ def tile_list_flock_page_alerts_kernel(
                 )
 
         def fetch(s):
-            picked = keep.tile([P, NX], F32, name="picked", tag=weave_tag(s + 2) if s + 2 < SLICES else "size%d" % (s - 1), align_bytes=64)
+            picked = keep.tile([P, NX], F32, name="picked", tag="size%d" % (s - 1), align_bytes=64)
             nc.vector.tensor_copy(picked[:], page[s][:].indirect(list3[:]))
             sizes[s] = keep.tile([P, NX], F32, name="size", tag="size%d" % s, align_bytes=64)
             nc.scalar.activation(sizes[s][:], picked[:], ACT.Abs)
@@ -268,23 +268,25 @@ def tile_list_flock_page_alerts_kernel(
         woven0 = []
         for s in range(SLICES):
             put(s)
-            if s + 2 < SLICES:
-                quantise_w1(s + 2)
+            if s == 0:
+                quantise_w1(2)
             fetch(s)
             if s + 2 < SLICES:
                 departure(s + 2)
                 square(s + 2)
+            if s + 3 < SLICES:
+                quantise_w1(s + 3)
             weigh(s)
             if s + 1 < SLICES:
                 feature(s + 1)
-                turn_page(s, ("a" if s + 2 < SLICES else "x", "b%d" % ((s + 1) % 2)), on_scalar)
+                turn_page(s, ("a", "b%d" % ((s + 1) % 2)), on_scalar)
             if s + 4 < SLICES:
                 weave_w1(s + 4)
             turn_x(s)
             if 4 <= s < 7:
                 woven0.append(turn_back((page_t[0, 0], page_t[0, 1], x_t[0])[s - 4], "raw%d" % (s - 4), both_on_scalar))
 
-        turn_page(SLICES - 1, ("x", "b1"), on_vector)
+        turn_page(SLICES - 1, ("a", "b1"), on_vector)
         codes = [
             keep.tile([P, 3, 512], U32, name="codes0", tag="row8", align_bytes=64),
             keep.tile([P, 3, 512], U32, name="codes1", align_bytes=64),
@@ -307,7 +309,7 @@ def tile_list_flock_page_alerts_kernel(
 
         for mt in range(T2 // P):
             hf, c = divmod(mt, 4)
-            e_bank = banks.tile([P, NX], F32, name="e_bank", tag=("a", "b0", "x", "b1")[mt % 4])
+            e_bank = banks.tile([P, NX], F32, name="e_bank", tag=("x", "b0", "a", "b1")[mt % 4])
             for b in reversed(range(PASSES)):
                 nc.tensor.matmul_mx(
                     out=e_bank[:],

@@ -95,6 +95,7 @@ def tile_list_flock_page_alerts_kernel(
         nc.sync.dma_start(list1[:], offs)
         load_w1(0, 0)
         load_scales(nc.sync, tab_s, tab_scales)
+        nc.sync.dma_start(list2[:], offs2)
         load_w1(0, 1)
         for a in range(PASSES):
             nc.sync.dma_start(out=tab_w[a][:], in_=tab_words[a].rearrange("p t i -> p (t i)").bitcast(I32))
@@ -104,7 +105,6 @@ def tile_list_flock_page_alerts_kernel(
         load_clutter(1)
         nc.sync.dma_start(out=gain[:], in_=wgs)
         load_page(0)
-        nc.sync.dma_start(list2[:], offs2)
         nc.sync.dma_start(list3[:], offs3)
         load_w1(1)
         load_clutter(2)
@@ -145,7 +145,7 @@ def tile_list_flock_page_alerts_kernel(
         w1_w = {}
 
         def quantise_w1(s):
-            w1_w[s] = keep.tile([P, PASSES * P], U32, name="w1_w", tag="size-1" if s == 3 else "w1_w%d" % s, align_bytes=64)
+            w1_w[s] = keep.tile([P, PASSES * P], U32, name="w1_w", tag=weave_tag(2) if s == 3 else "w1_w%d" % s, align_bytes=64)
             nc.vector.quantize_mx(out=w1_w[s][:].bitcast(FP8X4), scales=w1_s[s][:], in_=w1_woven[s][:].rearrange("p a n -> p (a n)"))
 
         for s in range(2):
@@ -220,7 +220,7 @@ def tile_list_flock_page_alerts_kernel(
                 )
 
         def fetch(s):
-            picked = keep.tile([P, NX], F32, name="picked", tag="size%d" % (s - 1), align_bytes=64)
+            picked = keep.tile([P, NX], F32, name="picked", tag="size%d" % (s - 1) if s else weave_tag(2), align_bytes=64)
             nc.vector.tensor_copy(picked[:], page[s][:].indirect(list3[:]))
             sizes[s] = keep.tile([P, NX], F32, name="size", tag="size%d" % s, align_bytes=64)
             nc.scalar.activation(sizes[s][:], picked[:], ACT.Abs)

from contextlib import ExitStack

import concourse.mybir as mybir
from concourse.masks import make_identity

K, T, S, H, T2, NX = 1024, 2048, 512, 1024, 1024, 512
FLOPS = 2 * (2 * K * H * S + H * T2 * NX)

F32 = mybir.dt.float32
BF16 = mybir.dt.bfloat16
I32 = mybir.dt.int32
U32 = mybir.dt.uint32
U16 = mybir.dt.uint16
U8 = mybir.dt.uint8
FP8X4 = mybir.dt.float8_e4m3fn_x4
FP4X4 = mybir.dt.float4_e2m1fn_x4
ALU = mybir.AluOpType
ACT = mybir.ActivationFunctionType

P = 128
PASSES = 2
SLICES = H // P
W4_CHUNKS = ((0, 2), (2, 8))
W1_CHUNKS = ((0, 2), (2, 4), (4, 6), (6, 8))


def tile_list_flock_page_alerts_kernel(
    tc, tab_words, tab_scales, offs, offs2, offs3, w1, clutter, w4_words, w4_scales, wgs, page0, hazard, slot, floors, out
):
    nc = tc.nc
    with ExitStack() as ctx:
        keep = ctx.enter_context(tc.tile_pool(name="keep", bufs=1))
        ring = ctx.enter_context(tc.tile_pool(name="ring", bufs=2))
        banks = ctx.enter_context(tc.psum_pool(name="banks", bufs=1))

        list1 = keep.tile([P, S // 16], U16, name="list1")
        list2 = keep.tile([P, S // 16], U16, name="list2")
        list3 = keep.tile([P, NX // 16], U16, name="list3")
        tab_w = [keep.tile([P, T], I32, name="tab_w%d" % a, tag="big%d" % a) for a in range(PASSES)]
        tab_s = keep.tile([P, PASSES, T], U8, name="tab_s")
        v_w = [keep.tile([P, S], U32, name="v_w%d" % a, align_bytes=64) for a in range(PASSES)]
        v_s = [keep.tile([P, S], U8, name="v_s%d" % a, align_bytes=64) for a in range(PASSES)]
        w4_w = [keep.tile([P, PASSES, 2 * P * (hi - lo)], U8, name="w4_w%d" % lo, align_bytes=64) for lo, hi in W4_CHUNKS]
        w4_s = keep.tile([P, PASSES, H], U8, name="w4_s", align_bytes=64)
        w1_raw = [
            [keep.tile([P, 4, P * (hi - lo)], F32, name="w1_raw", tag="raw%d" % (lo + a), align_bytes=64) for a in range(PASSES)]
            for lo, hi in W1_CHUNKS
        ]
        w1_s = [keep.tile([P, PASSES * P], U8, name="w1_s%d" % s, align_bytes=64) for s in range(SLICES)]
        clut = [keep.tile([P, S], F32, name="clut%d" % s, tag="row%d" % s, align_bytes=64) for s in range(SLICES)]
        gain = keep.tile([P, S], F32, name="gain")
        page = [keep.tile([P, T2], F32, name="page%d" % s) for s in range(SLICES)]
        vec_rows = keep.tile([P, P], F32, name="vec_rows")
        vec_cols = keep.tile([P, 16], F32, name="vec_cols")
        ident32 = keep.tile([P, P], F32, name="ident32")
        ident16 = keep.tile([P, P], BF16, name="ident16")
        page_s = [[keep.tile([P, 512], U8, name="page_s%d_%d" % (b, hf), align_bytes=64) for hf in range(2)] for b in range(PASSES)]
        x_s = [keep.tile([P, NX], U8, name="x_s%d" % b, align_bytes=64) for b in range(PASSES)]

        nc.gpsimd.memset(tab_s[:].rearrange("p a t -> p (a t)").bitcast(I32), 0)
        nc.vector.memset(w4_s[:].rearrange("p a t -> p (a t)").bitcast(I32), 0)

        def load_scales(queue, tile, src):
            for q in range(4):
                queue.dma_start(
                    out=tile[32 * q : 32 * q + 4, :, :].bitcast(I32),
                    in_=src[:, 4 * q : 4 * q + 4, :].rearrange("a q t -> q a t").bitcast(I32),
                )

        def load_w1(c, *passes):
            for a in passes or range(PASSES):
                nc.sync.dma_start(
                    out=w1_raw[c][a][:],
                    in_=w1[512 * a : 512 * (a + 1), P * W1_CHUNKS[c][0] : P * W1_CHUNKS[c][1]].rearrange("(p j) c -> p j c", j=4),
                )

        def load_clutter(s):
            nc.sync.dma_start(out=clut[s][:], in_=clutter[P * s : P * (s + 1), :])

        def load_page(s):
            nc.sync.dma_start(out=page[s][:], in_=page0[P * s : P * (s + 1), :])

        def load_w4(c):
            lo, hi = W4_CHUNKS[c]
            nc.sync.dma_start(
                out=w4_w[c][:].bitcast(I32),
                in_=w4_words.rearrange("a p n -> p a n")[:, :, 2 * P * lo : 2 * P * hi].bitcast(I32),
            )

        nc.gpsimd.memset(vec_rows[:], 0.0)
        make_identity(nc, ident32[:])
        make_identity(nc, ident16[:])
        nc.gpsimd.dma_start(out=vec_rows[0:8, :], in_=hazard.rearrange("(s p) -> s p", p=P))
        nc.gpsimd.dma_start(out=vec_rows[8:16, :], in_=slot.rearrange("(s p) -> s p", p=P))
        nc.sync.dma_start(list1[:], offs)
        load_w1(0, 0)
        load_scales(nc.sync, tab_s, tab_scales)
        nc.sync.dma_start(list2[:], offs2)
        load_w1(0, 1)
        for a in range(PASSES):
            nc.sync.dma_start(out=tab_w[a][:], in_=tab_words[a].rearrange("p t i -> p (t i)").bitcast(I32))
        load_scales(nc.sync, w4_s, w4_scales)
        load_w4(0)
        load_clutter(0)
        load_clutter(1)
        nc.sync.dma_start(out=gain[:], in_=wgs)
        load_page(0)
        nc.sync.dma_start(list3[:], offs3)
        load_w1(1)
        load_clutter(2)
        load_page(1)
        load_w4(1)
        load_clutter(3)
        load_w1(2)
        load_page(2)
        load_clutter(4)
        load_page(3)
        load_w1(3)
        for s in range(4, SLICES):
            if s + 1 < SLICES:
                load_clutter(s + 1)
            load_page(s)

        for a in range(PASSES):
            nc.vector.tensor_copy(v_s[a][:], tab_s[:, a, :].indirect(list1[:]))

        w1_woven = {}

        def diff_tag(s):
            return "row%d" % (s - 1 if s >= 2 else SLICES + 1 + s)

        def weave_tag(s):
            return diff_tag(s - 2) if s >= 2 else "weave%d" % s

        def weave_w1(s):
            c = [lo <= s < hi for lo, hi in W1_CHUNKS].index(True)
            c0 = P * (s - W1_CHUNKS[c][0])
            woven = keep.tile([P, PASSES, P * 4], BF16, name="w1_woven", tag=weave_tag(s), align_bytes=64)
            for a in range(PASSES):
                dst = woven[:, a, :].rearrange("p (c i j) -> p c j i", i=4, j=4)
                src = w1_raw[c][a][:, :, c0 : c0 + P].rearrange("p j (c i) -> p c j i", i=4)
                nc.scalar.copy(dst, src)
            w1_woven[s] = woven

        w1_w = {}

        def quantise_w1(s):
            w1_w[s] = keep.tile([P, PASSES * P], U32, name="w1_w", tag=weave_tag(2) if s == 3 else "w1_w%d" % s, align_bytes=64)
            nc.vector.quantize_mx(out=w1_w[s][:].bitcast(FP8X4), scales=w1_s[s][:], in_=w1_woven[s][:].rearrange("p a n -> p (a n)"))

        for s in range(2):
            weave_w1(s)
            quantise_w1(s)
        for a in range(PASSES):
            nc.vector.tensor_copy(v_w[a][:], tab_w[a][:].bitcast(U32).indirect(list1[:]))

        vec_bank = banks.tile([P, P], F32, name="vec_bank", tag="x")
        nc.tensor.transpose(vec_bank[:], vec_rows[:], ident32[:])
        nc.scalar.copy(vec_cols[:], vec_bank[:, 0:16])

        diffs = {}
        squares = {}
        feats = {}
        sizes = {}
        xs = {}
        page_t = {}
        x_t = {}

        def departure(s):
            a_bank = banks.tile([P, S], F32, name="a_bank", tag="c" if s == 1 else "a")
            for a in range(PASSES):
                nc.tensor.matmul_mx(
                    out=a_bank[:],
                    lhsT=w1_w[s][:, P * a : P * (a + 1)].bitcast(FP8X4),
                    lhsT_scale=w1_s[s][:, P * a : P * (a + 1)],
                    rhs=v_w[a][:].bitcast(FP8X4),
                    rhs_scale=v_s[a][:],
                    start=(a == 0),
                    stop=(a == PASSES - 1),
                )
            diffs[s] = keep.tile([P, S], F32, name="diff", tag=diff_tag(s), align_bytes=64)
            nc.vector.tensor_tensor(diffs[s][:], a_bank[:], clut[s][:], ALU.subtract)

        def square(s):
            squares[s] = ring.tile([P, S], F32, name="squared")
            nc.scalar.activation(squares[s][:], diffs[s][:], ACT.Square)

        def feature(s):
            c = [lo <= s < hi for lo, hi in W4_CHUNKS].index(True)
            at = s - W4_CHUNKS[c][0]
            b_bank = banks.tile([P, S], F32, name="b_bank", tag="b%d" % (s % 2))
            for a in range(PASSES):
                nc.tensor.matmul_mx(
                    out=b_bank[:],
                    lhsT=w4_w[c][:, a, 2 * P * at : 2 * P * (at + 1)].bitcast(FP4X4),
                    lhsT_scale=w4_s[:, a, P * s : P * (s + 1)],
                    rhs=v_w[a][:].bitcast(FP8X4),
                    rhs_scale=v_s[a][:],
                    start=(a == 0),
                    stop=(a == PASSES - 1),
                )
            feats[s] = keep.tile([P, S], F32, name="feat", tag="row%d" % (s + 1), align_bytes=64)
            nc.vector.tensor_tensor(feats[s][:], b_bank[:], squares[s][:], ALU.add)

        def put(s):
            nc.vector.tensor_tensor(page[s][:].indirect(list2[:]), feats[s][:], gain[:], ALU.mult)

        def turn_page(s, tags, copy):
            sl = s % 4
            for hf in range(2):
                if sl == 0:
                    page_t[s // 4, hf] = ring.tile([P, 2048], BF16, name="page_t", tag="page_t%d" % hf)
                bank = banks.tile([P, 4, P], F32, name="page_bank", tag=tags[hf])
                for mt in range(4):
                    c0 = P * (4 * hf + mt)
                    nc.tensor.transpose(bank[:, mt, :], page[s][:, c0 : c0 + P], ident32[:])
                copy(
                    page_t[s // 4, hf][:].rearrange("m (c u p e) -> m c u p e", c=4, u=2, e=2)[:, :, :, 32 * sl : 32 * sl + 32, :],
                    bank[:].rearrange("m c (p u e) -> m c u p e", u=2, e=2),
                )

        def fetch(s):
            picked = keep.tile([P, NX], F32, name="picked", tag="size%d" % (s - 1) if s else weave_tag(2), align_bytes=64)
            nc.vector.tensor_copy(picked[:], page[s][:].indirect(list3[:]))
            sizes[s] = keep.tile([P, NX], F32, name="size", tag="size%d" % s, align_bytes=64)
            nc.scalar.activation(sizes[s][:], picked[:], ACT.Abs)

        def weigh(s):
            xs[s] = ring.tile([P, NX], BF16, name="x")
            nc.scalar.activation(xs[s][:], sizes[s][:], ACT.Copy, scale=vec_cols[:, s : s + 1])

        def turn_x(s):
            sl = s % 4
            if sl == 0:
                x_t[s // 4] = ring.tile([P, 2048], BF16, name="x_t", tag="x_t")
            bank = banks.tile([P, 4, P], BF16, name="x_bank", tag="x" if s + 1 < SLICES else "c")
            for nt in range(4):
                nc.tensor.transpose(bank[:, nt, :], xs[s][:, P * nt : P * (nt + 1)], ident16[:])
            nc.scalar.copy(
                x_t[s // 4][:].bitcast(F32).rearrange("n (c u p) -> n c u p", c=4, u=2)[:, :, :, 32 * sl : 32 * sl + 32],
                bank[:].bitcast(F32).rearrange("n c (p u) -> n c u p", u=2),
            )

        def turn_back(turned, name, copies):
            words = turned[:].bitcast(F32).rearrange("m (c u p) -> m c u p", c=4, u=2)
            woven = keep.tile([P, 2048], BF16, name="woven", tag=name, align_bytes=64)
            woven_words = woven[:].bitcast(F32).rearrange("p (c m u) -> p c m u", c=4, u=2)
            for pair in range(2):
                bank = banks.tile([P, 2, 2, P], F32, name="back_bank", tag="back", bufs=3)
                for c in range(2):
                    for u in range(2):
                        nc.tensor.transpose(bank[:, c, u, :], words[:, 2 * pair + c, u, :], ident32[:])
                copies[pair](woven_words[:, 2 * pair : 2 * pair + 2, :, :], bank[:].rearrange("p c u m -> p c m u"))
            return woven

        def quantise(codes, scales, woven):
            nc.vector.quantize_mx(out=codes.bitcast(FP8X4), scales=scales[:], in_=woven[:])

        on_scalar = nc.scalar.copy
        on_vector = nc.vector.tensor_copy
        both_on_scalar = (on_scalar, on_scalar)
        for s in range(2):
            departure(s)
            square(s)
        feature(0)
        weave_w1(2)
        weave_w1(3)
        woven0 = []
        for s in range(SLICES):
            put(s)
            if s == 0:
                quantise_w1(2)
            fetch(s)
            if s + 2 < SLICES:
                departure(s + 2)
                square(s + 2)
            if s + 3 < SLICES:
                quantise_w1(s + 3)
            weigh(s)
            if s + 1 < SLICES:
                feature(s + 1)
                turn_page(s, ("a", "b%d" % ((s + 1) % 2)), on_scalar)
            if s + 4 < SLICES:
                weave_w1(s + 4)
            turn_x(s)
            if 4 <= s < 7:
                woven0.append(turn_back((page_t[0, 0], page_t[0, 1], x_t[0])[s - 4], "raw%d" % (s - 4), both_on_scalar))

        turn_page(SLICES - 1, ("a", "b1"), on_vector)
        codes = [
            keep.tile([P, 3, 512], U32, name="codes0", tag="row8", align_bytes=64),
            keep.tile([P, 3, 512], U32, name="codes1", align_bytes=64),
        ]
        for hf in range(2):
            quantise(codes[0][:, hf, :], page_s[0][hf], woven0[hf])
        quantise(codes[0][:, 2, :], x_s[0], woven0[2])
        page_woven = turn_back(page_t[1, 0], "raw3", both_on_scalar)
        x_woven = turn_back(x_t[1], "raw4", (on_scalar, on_vector))
        quantise(codes[1][:, 0, :], page_s[1][0], page_woven)
        quantise(codes[1][:, 2, :], x_s[1], x_woven)
        page_woven = turn_back(page_t[1, 1], "raw5", both_on_scalar)
        quantise(codes[1][:, 1, :], page_s[1][1], page_woven)

        floor = [keep.tile([P, 4, NX], F32, name="floor%d" % hf, tag="big%d" % hf) for hf in range(2)]
        for hf in range(2):
            nc.sync.dma_start(
                out=floor[hf][:], in_=floors[512 * hf : 512 * (hf + 1), :].rearrange("(s p) n -> p s n", p=P)
            )

        for mt in range(T2 // P):
            hf, c = divmod(mt, 4)
            e_bank = banks.tile([P, NX], F32, name="e_bank", tag=("x", "b0", "a", "b1")[mt % 4])
            for b in reversed(range(PASSES)):
                nc.tensor.matmul_mx(
                    out=e_bank[:],
                    lhsT=codes[b][:, hf, P * c : P * (c + 1)].bitcast(FP8X4),
                    lhsT_scale=page_s[b][hf][:, P * c : P * (c + 1)],
                    rhs=codes[b][:, 2, :].bitcast(FP8X4),
                    rhs_scale=x_s[b][:],
                    start=(b == PASSES - 1),
                    stop=(b == 0),
                )
            alert = keep.tile([P, NX], F32, name="alert%d" % mt)
            nc.vector.scalar_tensor_tensor(alert[:], e_bank[:], vec_cols[:, 8 + mt : 9 + mt], floor[hf][:, c, :], ALU.mult, ALU.max)
            nc.sync.dma_start(out=out[P * mt : P * (mt + 1), :], in_=alert[:])
